import numpy as np
import ml_dtypes


def mxq(x, axis, fmt="e4m3"):
    dtype, down = {"e4m3": (ml_dtypes.float8_e4m3fn, 7), "e5m2": (ml_dtypes.float8_e5m2, 14)}[fmt]
    v = np.moveaxis(np.asarray(x, np.float32).astype(ml_dtypes.bfloat16).astype(np.float64), axis, -1)
    blocks = v.reshape(v.shape[:-1] + (-1, 32))
    amax = np.abs(blocks).max(-1, keepdims=True)
    byte = np.maximum(np.where(amax > 0, np.frexp(amax)[1] - 1 + 127, 0) - down, 1)
    scale = np.exp2(byte - 127.0)
    codes = (blocks / scale).astype(np.float32).astype(dtype).astype(np.float64)
    return np.moveaxis((codes * scale).reshape(v.shape), -1, axis)


WIDE = False


def mx_kscale(k):
    if not WIDE:
        return np.ones(k)
    levels = np.array([10, -10, 5, -5, 0])
    if k % 512:
        return np.exp2(np.random.permutation(np.resize(levels, k // 32))).repeat(32)
    a = np.empty((k // 512, 16))
    for p in range(k // 512):
        a[p, :8] = np.random.permutation(np.resize(levels, 8))
        for g in range(8):
            far = levels[np.abs(levels - a[p, g]) >= 10]
            a[p, g + 8] = far[np.random.randint(len(far))]
    return np.exp2(a.ravel()).repeat(32)


def f64(x):
    return np.asarray(x).astype(np.float64)


def striped(idx):
    return np.tile(idx.reshape(-1, 16).T, (8, 1)).astype(np.uint16)


def unstriped(offs):
    return offs[:16].T.reshape(-1).astype(np.int64)


def striped8(idx):
    return np.concatenate([x.reshape(-1, 16).T for x in idx]).astype(np.uint16)


def runs(offs, k):
    lists = np.stack([offs[16 * r : 16 * r + 16].T.reshape(-1) for r in range(8)]).astype(np.int64)
    return lists[np.arange(k) % 512 // 64]


def pack_weight(w):
    k, n = w.shape
    w = f64(np.asarray(w, np.float32).astype(ml_dtypes.bfloat16)).reshape(k // 32, 32, n)
    amax = np.abs(w).max(1)
    byte = np.clip(np.where(amax > 0, np.frexp(amax)[1] - 1 + 127 - 7, 1), 1, 254)
    scaled = (w * np.exp2(127.0 - byte)[:, None, :]).reshape(k, n).astype(np.float32)
    words = np.ascontiguousarray(scaled.reshape(k // 512, 128, 4, n).transpose(0, 1, 3, 2)).astype(ml_dtypes.float8_e4m3fn).view(np.uint8)
    return words, np.ascontiguousarray(byte.astype(np.uint8).reshape(k // 512, 16, n))


def unpack_weight(words, scales):
    g, p, n, _ = words.shape
    vals = np.ascontiguousarray(words).view(ml_dtypes.float8_e4m3fn).astype(np.float64) * np.repeat(np.exp2(scales.astype(np.float64) - 127.0), 8, axis=1)[..., None]
    return vals.transpose(0, 1, 3, 2).reshape(g * 512, n)


K, T, S, N, H, W = 512, 2048, 512, 512, 512, 256


def setup_inputs():
    n = np.random.standard_normal
    s = mx_kscale(K)[:, None]
    u = mx_kscale(H)
    packed_xT = pack_weight(n((K, T)) * s)
    perm = np.stack([np.random.permutation(S) for _ in range(8)])
    return {
        "x_words": packed_xT[0],
        "x_scales": packed_xT[1],
        "w1": (n((K, H)) / np.sqrt(K) / s).astype(np.float32),
        "gn": (np.random.uniform(0.5, 1.5, (H, 1)) * u[:, None]).astype(np.float32),
        "w2": (n((H, N)) / np.sqrt(H) / u[:, None]).astype(np.float32),
        "w3": (n((K, N)) / np.sqrt(K) / s).astype(np.float32),
        "offs": striped(np.random.permutation(T)[:S]),
        "n1": striped8(perm[:, :W]),
        "n2": striped8(perm[:, W:]),
        "n3": striped8(np.stack([np.random.permutation(S) for _ in range(8)])),
        "two": striped(np.random.permutation(T)[:S]),
        "n4": striped(np.random.permutation(S)),
        "n5": striped(np.random.permutation(S)),
    }


def reference(x_words, x_scales, w1, gn, w2, w3, offs, n1, n2, n3, two, n4, n5):
    xq = unpack_weight(x_words, x_scales)[:, unstriped(offs)]
    y = mxq(f64(w1), 0, "e4m3").T @ xq
    pa = y[np.arange(H)[:, None], runs(n1, H)]
    pb = y[np.arange(H)[:, None], runs(n2, H)]
    ra = pa - (0.5 * pb)
    ds = y.copy()
    ds[np.arange(H)[:, None], runs(n2, H)] = ra
    z = f64(gn) * (ds - (0.5 * (ds[np.arange(H)[:, None], runs(n3, H)])))
    h = mxq(f64(w2), 0, "e4m3").T @ mxq(z, 0, "e4m3")
    x_two = unpack_weight(x_words, x_scales)[:, unstriped(two)]
    d = mxq(f64(w3), 0, "e4m3").T @ x_two
    return h[:, unstriped(n4)] - (np.tanh(d) * d[:, unstriped(n5)])

@@ -1,0 +1,221 @@
+from contextlib import ExitStack
+
+import concourse.mybir as mybir
+
+K, T, S, N, H, W = 512, 2048, 512, 512, 512, 256
+FLOPS = 2 * (K * H * S + H * N * S + K * N * S)
+
+F32 = mybir.dt.float32
+BF16 = mybir.dt.bfloat16
+I32 = mybir.dt.int32
+U32 = mybir.dt.uint32
+U16 = mybir.dt.uint16
+U8 = mybir.dt.uint8
+FP8X4 = mybir.dt.float8_e4m3fn_x4
+COPY = mybir.ActivationFunctionType.Copy
+TANH = mybir.ActivationFunctionType.Tanh
+ADD = mybir.AluOpType.add
+MULT = mybir.AluOpType.mult
+SUB = mybir.AluOpType.subtract
+
+P = 128
+PACK = 4
+HALF = S // 2
+LCOL = HALF // 16
+PAD = 16
+
+
+def tile_picked_latesoftbfoldd_none_p_kernel(tc, x_words, x_scales, w1, gn, w2, w3, offs, n1, n2, n3, two, n4, n5, out):
+    nc = tc.nc
+    with ExitStack() as ctx:
+        held = ctx.enter_context(tc.tile_pool(name="held", bufs=1))
+        psum = ctx.enter_context(tc.psum_pool(name="psum", bufs=1))
+
+        def load_list(name, src):
+            tile = held.tile(list(src.shape), U16, name=name)
+            nc.sync.dma_start(tile[:], src)
+            return tile
+
+        def load_weight(name, src):
+            tile = held.tile([P, PACK, src.shape[1]], F32, name=name)
+            nc.sync.dma_start(tile[:], src.rearrange("(p j) c -> p j c", j=PACK))
+            return tile
+
+        def half(h):
+            return slice(h * HALF, (h + 1) * HALF)
+
+        def list_half(tile, h):
+            return tile[:, h * LCOL : (h + 1) * LCOL]
+
+        xs = held.tile([P, T], U8, name="xs")
+        nc.vector.memset(xs[:].bitcast(I32), 0)
+        w1_rows = w1.rearrange("(p j) c -> p j c", j=PACK)
+        w1_raw = [held.tile([P, PACK, H // 2], F32, name=f"w1_raw{h}") for h in range(2)]
+        nc.sync.dma_start(w1_raw[0][:], w1_rows[:, :, : H // 2])
+        for q in range(4):
+            nc.sync.dma_start(xs[32 * q : 32 * q + 4, :].bitcast(I32), x_scales[0, 4 * q : 4 * q + 4, :].bitcast(I32))
+        offs_t = load_list("offs_t", offs)
+        two_t = load_list("two_t", two)
+        xw = held.tile([P, T], I32, name="xw")
+        nc.sync.dma_start(xw[:], x_words[0].rearrange("p n t -> p (n t)").bitcast(I32))
+        nc.sync.dma_start(w1_raw[1][:], w1_rows[:, :, H // 2 :])
+        gn_t = held.tile([P, PACK], F32, name="gn_t")
+        nc.sync.dma_start(gn_t[:], gn.rearrange("(p t) o -> p (t o)", t=PACK))
+        n1_t = load_list("n1_t", n1)
+        n2_t = load_list("n2_t", n2)
+        w3_raw = load_weight("w3_raw", w3)
+        n3_t = load_list("n3_t", n3)
+        n5_t = load_list("n5_t", n5)
+        w2_raw = load_weight("w2_raw", w2)
+        n4_t = load_list("n4_t", n4)
+
+        def window(name, spare):
+            tile = held.tile([P, S + spare], F32, name=name)
+            nc.gpsimd.memset(tile[:, S:], 0.0)
+            return tile
+
+        ds = [window(f"ds{t}", S) for t in range(PACK)]
+        d_sb = [window(f"d{m}", PAD) for m in range(4)]
+        h_sb = [window(f"h{m}", PAD) for m in range(4)]
+
+        def mx_tiles(name, width, tags=("", "")):
+            codes = held.tile([P, width], U32, name=name + "_codes", tag=tags[0] or name + "_codes", align_bytes=64)
+            scales = held.tile([P, width], U8, name=name + "_scales", tag=tags[1] or name + "_scales", align_bytes=64)
+            return codes, scales
+
+        def quantise(mx, cols, src):
+            nc.vector.quantize_mx(out=mx[0][:, cols].bitcast(FP8X4), scales=mx[1][:, cols], in_=src)
+
+        def product(acc, stat, m, mov, cols):
+            rows = slice(m * P, (m + 1) * P)
+            nc.tensor.matmul_mx(acc, lhsT=stat[0][:, rows].bitcast(FP8X4), lhsT_scale=stat[1][:, rows],
+                                rhs=mov[0][:, cols].bitcast(FP8X4), rhs_scale=mov[1][:, cols], start=True, stop=True)
+
+        xa = mx_tiles("xa", S)
+        xb_scales = held.tile([P, S], U8, name="xb_scales", align_bytes=64)
+        nc.vector.tensor_copy(xa[1][:], xs[:].indirect(offs_t[:]))
+        nc.vector.tensor_copy(xb_scales[:], xs[:].indirect(two_t[:]))
+        nc.vector.tensor_copy(xa[0][:], xw[:].bitcast(U32).indirect(offs_t[:]))
+
+        w1_b = held.tile([P, PACK, P, PACK], BF16, name="w1_b", align_bytes=64)
+
+        def deal(h, lo, hi):
+            dst = w1_b[:, :, 64 * h + lo : 64 * h + hi, :].rearrange("p t m j -> p m j t")
+            src = w1_raw[h][:, :, PACK * lo : PACK * hi].rearrange("p j (m t) -> p m j t", t=PACK)
+            return dst, src
+
+        nc.scalar.activation(*deal(0, 0, 64), COPY)
+        nc.vector.tensor_copy(*deal(1, 0, 40))
+        nc.scalar.activation(*deal(1, 40, 64), COPY)
+        w1_q = mx_tiles("w1q", H)
+        banks = [psum.tile([P, S], F32, name=f"ybank{t}", tag=f"bank{t}") for t in range(PACK)]
+        for t in range(PACK):
+            quantise(w1_q, slice(t * P, (t + 1) * P), w1_b[:, t, :, :].rearrange("p m j -> p (m j)"))
+            product(banks[t][:], w1_q, t, xa, slice(0, S))
+        xb_codes = held.tile([P, S], U32, name="xb_codes", tag="w1_b", align_bytes=64)
+        xb = (xb_codes, xb_scales)
+
+        def pick_two():
+            nc.vector.tensor_copy(xb[0][:], xw[:].bitcast(U32).indirect(two_t[:]))
+
+        def interleave(dst, src):
+            nc.vector.tensor_copy(dst.rearrange("p (c i t) -> p c t i", i=4, t=PACK),
+                                  src.rearrange("p t (c i) -> p c t i", i=4))
+
+        def weight(name, raw):
+            mx = mx_tiles(name, N)
+            wbs = [held.tile([P, PACK * HALF], BF16, name=f"{name}_b{h}", align_bytes=64) for h in range(2)]
+            for h in range(2):
+                interleave(wbs[h][:], raw[:, :, half(h)])
+            for h in range(2):
+                quantise(mx, half(h), wbs[h][:])
+            return mx
+
+        zb = held.tile([P, PACK, S], BF16, name="zb")
+
+        def fold(t):
+            nc.scalar.activation(ds[t][:, :S], banks[t][:], COPY, scale=gn_t[:, t : t + 1])
+            pa = held.tile([P, W], F32, name=f"pa{t}")
+            pb = held.tile([P, W], F32, name=f"pb{t}")
+            nc.scalar.activation(pa[:], ds[t][:].indirect(n1_t[:]), COPY)
+            if t in (1,2,3):
+                nc.scalar.activation(pb[:], ds[t][:].indirect(n2_t[:]), COPY, scale=-0.5)
+            else:
+                nc.vector.tensor_scalar(pb[:], ds[t][:].indirect(n2_t[:]), -0.5, 0.0, MULT, ADD)
+            nc.vector.tensor_tensor(ds[t][:].indirect(n2_t[:]), pa[:], pb[:], ADD)
+
+        fars = []
+
+        def mix(t, pieces):
+            far = held.tile([P, S], F32, name=f"far{t}")
+            width = S // pieces
+            for h in range(pieces):
+                cols = slice(h * width, (h + 1) * width)
+                nc.scalar.activation(far[:, cols], ds[t][:].indirect(n3_t[:, h * width // 16 : (h + 1) * width // 16]), COPY, scale=-0.5)
+                nc.vector.tensor_tensor(zb[:, t, cols], ds[t][:, cols], far[:, cols], ADD)
+
+        def leave(dst, bank, on_scalar):
+            if on_scalar:
+                nc.scalar.activation(dst[:, :S], bank[:], COPY)
+            else:
+                nc.vector.tensor_copy(dst[:, :S], bank[:])
+
+        gates = []
+
+        def second(m, tag=""):
+            th = held.tile([P, S], F32, name=f"th{m}")
+            dg = held.tile([P, S], F32, name=f"dg{m}", tag=tag or f"dg{m}")
+            gate = held.tile([P, S], F32, name=f"gate{m}")
+            nc.scalar.activation(th[:], dbanks[m][:], TANH)
+            nc.scalar.activation(dg[:], d_sb[m][:].indirect(n5_t[:]), COPY)
+            gates.append((gate, th, dg))
+
+        def gate_product(m):
+            gate, th, dg = gates[m]
+            nc.vector.tensor_tensor(gate[:], th[:], dg[:], MULT)
+
+        fold(0)
+        pick_two()
+        w3_q = weight("w3q", w3_raw)
+        dbanks = [psum.tile([P, S], F32, name=f"dbank{m}", tag=f"bank{4 + m}") for m in range(4)]
+        for m in range(4):
+            product(dbanks[m][:], w3_q, m, xb, slice(0, S))
+        fold(1)
+        mix(0, 1)
+        fold(2)
+        mix(1, 1)
+        fold(3)
+        w2_q = weight("w2q", w2_raw)
+        mix(2, 1)
+        mix(3, 2)
+        leave(d_sb[0], dbanks[0], True)
+        leave(d_sb[1], dbanks[1], True)
+
+        z_q = [mx_tiles(f"zq{h}", HALF) for h in range(2)]
+        hbanks = [psum.tile([P, S], F32, name=f"hbank{m}", tag=f"bank{m}") for m in range(4)]
+        zi = [held.tile([P, PACK * HALF], BF16, name=f"zi{h}", align_bytes=64) for h in range(2)]
+        for h in range(2):
+            interleave(zi[h][:], zb[:, :, half(h)])
+        for h in range(2):
+            quantise(z_q[h], slice(0, HALF), zi[h][:])
+            for m in range(4):
+                product(hbanks[m][:, half(h)], w2_q, m, z_q[h], slice(0, HALF))
+        leave(h_sb[0], hbanks[0], False)
+        leave(d_sb[2], dbanks[2], False)
+        leave(d_sb[3], dbanks[3], False)
+        for m in range(1, 4):
+            leave(h_sb[m], hbanks[m], False)
+        for m in range(4):
+            second(m)
+
+        for m in range(4):
+            gate_product(m)
+            pieces = 2 if m == 3 else 1
+            width = S // pieces
+            for h in range(pieces):
+                cols = slice(h * width, (h + 1) * width)
+                hg = held.tile([P, width], F32, name=f"hg{m}_{h}")
+                res = held.tile([P, width], F32, name=f"res{m}_{h}")
+                nc.scalar.activation(hg[:], h_sb[m][:].indirect(n4_t[:, h * width // 16 : (h + 1) * width // 16]), COPY)
+                nc.vector.tensor_tensor(res[:], hg[:], gates[m][0][:, cols], SUB)
+                nc.sync.dma_start(out[m * P : (m + 1) * P, cols], res[:])

@@ -71,7 +71,7 @@ def tile_picked_latesoftbfoldd_none_p_kernel(tc, x_words, x_scales, w1, gn, w2, 
 
         def window(name, spare):
             tile = held.tile([P, S + spare], F32, name=name)
-            nc.gpsimd.memset(tile[:, S:], 0.0)
+            nc.vector.memset(tile[:, S:], 0.0)
             return tile
 
         ds = [window(f"ds{t}", S) for t in range(PACK)]
@@ -99,16 +99,17 @@ def tile_picked_latesoftbfoldd_none_p_kernel(tc, x_words, x_scales, w1, gn, w2, 
 
         w1_b = held.tile([P, PACK, P, PACK], BF16, name="w1_b", align_bytes=64)
 
-        def deal(h, lo, hi):
-            dst = w1_b[:, :, 64 * h + lo : 64 * h + hi, :].rearrange("p t m j -> p m j t")
-            src = w1_raw[h][:, :, PACK * lo : PACK * hi].rearrange("p j (m t) -> p m j t", t=PACK)
+        def deal(h, planes):
+            dst = w1_b[:, planes, 64 * h : 64 * h + 64, :]
+            src = w1_raw[h][:].rearrange("p j (m t) -> p t m j", t=PACK)[:, planes, :, :]
             return dst, src
 
-        nc.scalar.activation(*deal(0, 0, 64), COPY)
-        nc.vector.tensor_copy(*deal(1, 0, 40))
-        nc.scalar.activation(*deal(1, 40, 64), COPY)
+        nc.scalar.activation(*deal(0, slice(0, PACK)), COPY)
         w1_q = mx_tiles("w1q", H)
         banks = [psum.tile([P, S], F32, name=f"ybank{t}", tag=f"bank{t}") for t in range(PACK)]
+        for t in range(2):
+            nc.vector.tensor_copy(*deal(1, slice(t, t + 1)))
+            nc.scalar.activation(*deal(1, slice(t + 2, t + 3)), COPY)
         for t in range(PACK):
             quantise(w1_q, slice(t * P, (t + 1) * P), w1_b[:, t, :, :].rearrange("p m j -> p (m j)"))
             product(banks[t][:], w1_q, t, xa, slice(0, S))
@@ -187,9 +188,13 @@ def tile_picked_latesoftbfoldd_none_p_kernel(tc, x_words, x_scales, w1, gn, w2, 
         fold(3)
         w2_q = weight("w2q", w2_raw)
         mix(2, 1)
-        mix(3, 2)
         leave(d_sb[0], dbanks[0], True)
+        second(0)
+        mix(3, 2)
         leave(d_sb[1], dbanks[1], True)
+        second(1)
+        leave(d_sb[2], dbanks[2], True)
+        second(2)
 
         z_q = [mx_tiles(f"zq{h}", HALF) for h in range(2)]
         hbanks = [psum.tile([P, S], F32, name=f"hbank{m}", tag=f"bank{m}") for m in range(4)]
@@ -200,16 +205,14 @@ def tile_picked_latesoftbfoldd_none_p_kernel(tc, x_words, x_scales, w1, gn, w2, 
             quantise(z_q[h], slice(0, HALF), zi[h][:])
             for m in range(4):
                 product(hbanks[m][:, half(h)], w2_q, m, z_q[h], slice(0, HALF))
-        leave(h_sb[0], hbanks[0], False)
-        leave(d_sb[2], dbanks[2], False)
         leave(d_sb[3], dbanks[3], False)
-        for m in range(1, 4):
-            leave(h_sb[m], hbanks[m], False)
+        second(3)
         for m in range(4):
-            second(m)
+            leave(h_sb[m], hbanks[m], False)
 
         for m in range(4):
             gate_product(m)
+        for m in range(4):
             pieces = 2 if m == 3 else 1
             width = S // pieces
             for h in range(pieces):

from contextlib import ExitStack

import concourse.mybir as mybir

K, T, S, N, H, W = 512, 2048, 512, 512, 512, 256
FLOPS = 2 * (K * H * S + H * N * S + K * N * S)

F32 = mybir.dt.float32
BF16 = mybir.dt.bfloat16
I32 = mybir.dt.int32
U32 = mybir.dt.uint32
U16 = mybir.dt.uint16
U8 = mybir.dt.uint8
FP8X4 = mybir.dt.float8_e4m3fn_x4
COPY = mybir.ActivationFunctionType.Copy
TANH = mybir.ActivationFunctionType.Tanh
ADD = mybir.AluOpType.add
MULT = mybir.AluOpType.mult
SUB = mybir.AluOpType.subtract

P = 128
PACK = 4
HALF = S // 2
LCOL = HALF // 16
PAD = 16


def tile_picked_latesoftbfoldd_none_p_kernel(tc, x_words, x_scales, w1, gn, w2, w3, offs, n1, n2, n3, two, n4, n5, out):
    nc = tc.nc
    with ExitStack() as ctx:
        held = ctx.enter_context(tc.tile_pool(name="held", bufs=1))
        psum = ctx.enter_context(tc.psum_pool(name="psum", bufs=1))

        def load_list(name, src):
            tile = held.tile(list(src.shape), U16, name=name)
            nc.sync.dma_start(tile[:], src)
            return tile

        def load_weight(name, src):
            tile = held.tile([P, PACK, src.shape[1]], F32, name=name)
            nc.sync.dma_start(tile[:], src.rearrange("(p j) c -> p j c", j=PACK))
            return tile

        def half(h):
            return slice(h * HALF, (h + 1) * HALF)

        def list_half(tile, h):
            return tile[:, h * LCOL : (h + 1) * LCOL]

        xs = held.tile([P, T], U8, name="xs")
        nc.vector.memset(xs[:].bitcast(I32), 0)
        w1_rows = w1.rearrange("(p j) c -> p j c", j=PACK)
        w1_raw = [held.tile([P, PACK, H // 2], F32, name=f"w1_raw{h}") for h in range(2)]
        nc.sync.dma_start(w1_raw[0][:], w1_rows[:, :, : H // 2])
        for q in range(4):
            nc.sync.dma_start(xs[32 * q : 32 * q + 4, :].bitcast(I32), x_scales[0, 4 * q : 4 * q + 4, :].bitcast(I32))
        offs_t = load_list("offs_t", offs)
        two_t = load_list("two_t", two)
        xw = held.tile([P, T], I32, name="xw")
        nc.sync.dma_start(xw[:], x_words[0].rearrange("p n t -> p (n t)").bitcast(I32))
        nc.sync.dma_start(w1_raw[1][:], w1_rows[:, :, H // 2 :])
        gn_t = held.tile([P, PACK], F32, name="gn_t")
        nc.sync.dma_start(gn_t[:], gn.rearrange("(p t) o -> p (t o)", t=PACK))
        n1_t = load_list("n1_t", n1)
        n2_t = load_list("n2_t", n2)
        w3_raw = load_weight("w3_raw", w3)
        n3_t = load_list("n3_t", n3)
        n5_t = load_list("n5_t", n5)
        w2_raw = load_weight("w2_raw", w2)
        n4_t = load_list("n4_t", n4)

        def window(name, spare):
            tile = held.tile([P, S + spare], F32, name=name)
            nc.vector.memset(tile[:, S:], 0.0)
            return tile

        ds = [window(f"ds{t}", S) for t in range(PACK)]
        d_sb = [window(f"d{m}", PAD) for m in range(4)]
        h_sb = [window(f"h{m}", PAD) for m in range(4)]

        def mx_tiles(name, width, tags=("", "")):
            codes = held.tile([P, width], U32, name=name + "_codes", tag=tags[0] or name + "_codes", align_bytes=64)
            scales = held.tile([P, width], U8, name=name + "_scales", tag=tags[1] or name + "_scales", align_bytes=64)
            return codes, scales

        def quantise(mx, cols, src):
            nc.vector.quantize_mx(out=mx[0][:, cols].bitcast(FP8X4), scales=mx[1][:, cols], in_=src)

        def product(acc, stat, m, mov, cols):
            rows = slice(m * P, (m + 1) * P)
            nc.tensor.matmul_mx(acc, lhsT=stat[0][:, rows].bitcast(FP8X4), lhsT_scale=stat[1][:, rows],
                                rhs=mov[0][:, cols].bitcast(FP8X4), rhs_scale=mov[1][:, cols], start=True, stop=True)

        xa = mx_tiles("xa", S)
        xb_scales = held.tile([P, S], U8, name="xb_scales", align_bytes=64)
        nc.vector.tensor_copy(xa[1][:], xs[:].indirect(offs_t[:]))
        nc.vector.tensor_copy(xb_scales[:], xs[:].indirect(two_t[:]))
        nc.vector.tensor_copy(xa[0][:], xw[:].bitcast(U32).indirect(offs_t[:]))

        w1_b = held.tile([P, PACK, P, PACK], BF16, name="w1_b", align_bytes=64)

        def deal(h, planes):
            dst = w1_b[:, planes, 64 * h : 64 * h + 64, :]
            src = w1_raw[h][:].rearrange("p j (m t) -> p t m j", t=PACK)[:, planes, :, :]
            return dst, src

        nc.scalar.activation(*deal(0, slice(0, PACK)), COPY)
        w1_q = mx_tiles("w1q", H)
        banks = [psum.tile([P, S], F32, name=f"ybank{t}", tag=f"bank{t}") for t in range(PACK)]
        for t in range(2):
            nc.vector.tensor_copy(*deal(1, slice(t, t + 1)))
            nc.scalar.activation(*deal(1, slice(t + 2, t + 3)), COPY)
        for t in range(PACK):
            quantise(w1_q, slice(t * P, (t + 1) * P), w1_b[:, t, :, :].rearrange("p m j -> p (m j)"))
            product(banks[t][:], w1_q, t, xa, slice(0, S))
        xb_codes = held.tile([P, S], U32, name="xb_codes", tag="w1_b", align_bytes=64)
        xb = (xb_codes, xb_scales)

        def pick_two():
            nc.vector.tensor_copy(xb[0][:], xw[:].bitcast(U32).indirect(two_t[:]))

        def interleave(dst, src):
            nc.vector.tensor_copy(dst.rearrange("p (c i t) -> p c t i", i=4, t=PACK),
                                  src.rearrange("p t (c i) -> p c t i", i=4))

        def weight(name, raw):
            mx = mx_tiles(name, N)
            wbs = [held.tile([P, PACK * HALF], BF16, name=f"{name}_b{h}", align_bytes=64) for h in range(2)]
            for h in range(2):
                interleave(wbs[h][:], raw[:, :, half(h)])
            for h in range(2):
                quantise(mx, half(h), wbs[h][:])
            return mx

        zb = held.tile([P, PACK, S], BF16, name="zb")

        def fold(t):
            nc.scalar.activation(ds[t][:, :S], banks[t][:], COPY, scale=gn_t[:, t : t + 1])
            pa = held.tile([P, W], F32, name=f"pa{t}")
            pb = held.tile([P, W], F32, name=f"pb{t}")
            nc.scalar.activation(pa[:], ds[t][:].indirect(n1_t[:]), COPY)
            if t in (1,2,3):
                nc.scalar.activation(pb[:], ds[t][:].indirect(n2_t[:]), COPY, scale=-0.5)
            else:
                nc.vector.tensor_scalar(pb[:], ds[t][:].indirect(n2_t[:]), -0.5, 0.0, MULT, ADD)
            nc.vector.tensor_tensor(ds[t][:].indirect(n2_t[:]), pa[:], pb[:], ADD)

        fars = []

        def mix(t, pieces):
            far = held.tile([P, S], F32, name=f"far{t}")
            width = S // pieces
            for h in range(pieces):
                cols = slice(h * width, (h + 1) * width)
                nc.scalar.activation(far[:, cols], ds[t][:].indirect(n3_t[:, h * width // 16 : (h + 1) * width // 16]), COPY, scale=-0.5)
                nc.vector.tensor_tensor(zb[:, t, cols], ds[t][:, cols], far[:, cols], ADD)

        def leave(dst, bank, on_scalar):
            if on_scalar:
                nc.scalar.activation(dst[:, :S], bank[:], COPY)
            else:
                nc.vector.tensor_copy(dst[:, :S], bank[:])

        gates = []

        def second(m, tag=""):
            th = held.tile([P, S], F32, name=f"th{m}")
            dg = held.tile([P, S], F32, name=f"dg{m}", tag=tag or f"dg{m}")
            gate = held.tile([P, S], F32, name=f"gate{m}")
            nc.scalar.activation(th[:], dbanks[m][:], TANH)
            nc.scalar.activation(dg[:], d_sb[m][:].indirect(n5_t[:]), COPY)
            gates.append((gate, th, dg))

        def gate_product(m):
            gate, th, dg = gates[m]
            nc.vector.tensor_tensor(gate[:], th[:], dg[:], MULT)

        fold(0)
        pick_two()
        w3_q = weight("w3q", w3_raw)
        dbanks = [psum.tile([P, S], F32, name=f"dbank{m}", tag=f"bank{4 + m}") for m in range(4)]
        for m in range(4):
            product(dbanks[m][:], w3_q, m, xb, slice(0, S))
        fold(1)
        mix(0, 1)
        fold(2)
        mix(1, 1)
        fold(3)
        w2_q = weight("w2q", w2_raw)
        mix(2, 1)
        leave(d_sb[0], dbanks[0], True)
        second(0)
        mix(3, 2)
        leave(d_sb[1], dbanks[1], True)
        second(1)
        leave(d_sb[2], dbanks[2], True)
        second(2)

        z_q = [mx_tiles(f"zq{h}", HALF) for h in range(2)]
        hbanks = [psum.tile([P, S], F32, name=f"hbank{m}", tag=f"bank{m}") for m in range(4)]
        zi = [held.tile([P, PACK * HALF], BF16, name=f"zi{h}", align_bytes=64) for h in range(2)]
        for h in range(2):
            interleave(zi[h][:], zb[:, :, half(h)])
        for h in range(2):
            quantise(z_q[h], slice(0, HALF), zi[h][:])
            for m in range(4):
                product(hbanks[m][:, half(h)], w2_q, m, z_q[h], slice(0, HALF))
        leave(d_sb[3], dbanks[3], False)
        second(3)
        for m in range(4):
            leave(h_sb[m], hbanks[m], False)

        for m in range(4):
            gate_product(m)
        for m in range(4):
            pieces = 2 if m == 3 else 1
            width = S // pieces
            for h in range(pieces):
                cols = slice(h * width, (h + 1) * width)
                hg = held.tile([P, width], F32, name=f"hg{m}_{h}")
                res = held.tile([P, width], F32, name=f"res{m}_{h}")
                nc.scalar.activation(hg[:], h_sb[m][:].indirect(n4_t[:, h * width // 16 : (h + 1) * width // 16]), COPY)
                nc.vector.tensor_tensor(res[:], hg[:], gates[m][0][:, cols], SUB)
                nc.sync.dma_start(out[m * P : (m + 1) * P, cols], res[:])
